import numpy as np
import ml_dtypes


def mxq(x, axis, fmt="e4m3"):
    dtype, down = {"e4m3": (ml_dtypes.float8_e4m3fn, 7), "e5m2": (ml_dtypes.float8_e5m2, 14)}[fmt]
    v = np.moveaxis(np.asarray(x, np.float32).astype(ml_dtypes.bfloat16).astype(np.float64), axis, -1)
    blocks = v.reshape(v.shape[:-1] + (-1, 32))
    amax = np.abs(blocks).max(-1, keepdims=True)
    byte = np.maximum(np.where(amax > 0, np.frexp(amax)[1] - 1 + 127, 0) - down, 1)
    scale = np.exp2(byte - 127.0)
    codes = (blocks / scale).astype(np.float32).astype(dtype).astype(np.float64)
    return np.moveaxis((codes * scale).reshape(v.shape), -1, axis)


WIDE = False


def mx_kscale(k, group=512):
    if not WIDE:
        return np.ones(k)
    levels = np.array([10, -10, 5, -5, 0])
    if group != 512:
        return np.exp2(np.random.permutation(np.resize(levels, k // group))).repeat(group)
    if k % 512:
        return np.exp2(np.random.permutation(np.resize(levels, k // 32))).repeat(32)
    a = np.empty((k // 512, 16))
    for p in range(k // 512):
        a[p, :8] = np.random.permutation(np.resize(levels, 8))
        for g in range(8):
            far = levels[np.abs(levels - a[p, g]) >= 10]
            a[p, g + 8] = far[np.random.randint(len(far))]
    return np.exp2(a.ravel()).repeat(32)


def f64(x):
    return np.asarray(x).astype(np.float64)


def gelu(v):
    return 0.5 * v * (1.0 + np.tanh(0.7978845608028654 * (v + 0.044715 * v ** 3)))


G, D, M, N = 4, 256, 256, 512


def setup_inputs():
    n = np.random.standard_normal
    s = mx_kscale(D, 0)[:, None]
    return {
        "x": (n((G, D, N)) * s).astype(np.float32),
        "w": (n((G, D, M)) / np.sqrt(D) / s).astype(np.float32),
        "b": (0.5 * n((G, M, 1))).astype(np.float32),
        "r": n((G, M, N)).astype(np.float32),
    }


def reference(x, w, b, r):
    xq = mxq(f64(x), 1, "e4m3")
    y = mxq(f64(w), 1, "e4m3").transpose(0, 2, 1) @ xq
    y = y + f64(b)
    y = gelu(y)
    y = y + f64(r)
    return y

@@ -1,0 +1,127 @@
+from contextlib import ExitStack
+
+import concourse.mybir as mybir
+
+G, D, M, N = 4, 256, 256, 512
+
+F32 = mybir.dt.float32
+BF16 = mybir.dt.bfloat16
+U32 = mybir.dt.uint32
+U8 = mybir.dt.uint8
+FP8X4 = mybir.dt.float8_e4m3fn_x4
+GELU = mybir.ActivationFunctionType.Gelu_apprx_tanh
+
+P = 128
+PACK = 4
+ROWS = D // PACK
+SIDE = P // ROWS
+PAIRS = G // SIDE
+TILES = M // P
+BIAS_PITCH = 8
+
+FLOPS = 2 * G * D * M * N
+
+
+def tile_rows_glin_gelu_bias_res_kernel(tc, x, w, b, r, out):
+    nc = tc.nc
+    x_rows = x.flatten_outer_dims().rearrange("(q p j) n -> q p j n", p=P, j=PACK)
+    w_rows = w.flatten_outer_dims().rearrange("(q p j) m -> q p j m", p=P, j=PACK)
+    b_rows = b.rearrange("g (p t) o -> p g (t o)", t=TILES)
+    r_rows = r.rearrange("g (p t) n -> g p t n", t=TILES)
+    out_rows = out.rearrange("g (p t) n -> g p t n", t=TILES)
+
+    with ExitStack() as ctx:
+        sb = ctx.enter_context(tc.tile_pool(name="sb", bufs=1))
+        ps = ctx.enter_context(tc.psum_pool(name="ps", bufs=1))
+        ctx.enter_context(tc.manual_schedule())
+
+        bias = sb.tile([P, G, BIAS_PITCH], F32, name="bias")
+        x_raw = [sb.tile([P, PACK, N], F32, name="x_raw%d" % q, align_bytes=64) for q in range(PAIRS)]
+        w_raw = [sb.tile([P, PACK, M], F32, name="w_raw%d" % q, align_bytes=64) for q in range(PAIRS)]
+        x_bf = [sb.tile([P, N, PACK], BF16, name="x_bf%d" % q, align_bytes=64) for q in range(PAIRS)]
+        w_bf = [sb.tile([P, M, PACK], BF16, name="w_bf%d" % q, align_bytes=64) for q in range(PAIRS)]
+        x_codes = [sb.tile([P, N], U32, name="x_codes%d" % q, align_bytes=64) for q in range(PAIRS)]
+        w_codes = [sb.tile([P, M], U32, name="w_codes%d" % q, align_bytes=64) for q in range(PAIRS)]
+        x_scales = [sb.tile([P, N], U8, name="x_scales%d" % q, align_bytes=64) for q in range(PAIRS)]
+        w_scales = [sb.tile([P, M], U8, name="w_scales%d" % q, align_bytes=64) for q in range(PAIRS)]
+        res = [sb.tile([P, TILES, N], F32, name="res%d" % g, align_bytes=64) for g in range(G)]
+        act = [sb.tile([P, TILES, N], F32, name="act%d" % g, align_bytes=64) for g in range(G)]
+        sums = [[ps.tile([P, N], F32, name="sums%d_%d" % (g, t)) for t in range(TILES)] for g in range(G)]
+
+        def pack_x(q, cols):
+            nc.vector.tensor_copy(out=x_bf[q][:, cols, :], in_=x_raw[q][:, :, cols].rearrange("p j n -> p n j"))
+
+        def quantize_x(q, cols):
+            nc.vector.quantize_mx(
+                out=x_codes[q][:, cols].bitcast(FP8X4),
+                scales=x_scales[q][:, cols],
+                in_=x_bf[q][:, cols, :].rearrange("p n j -> p (n j)"),
+            )
+
+        def pack_w(q, tiles, copy):
+            copy(
+                out=w_bf[q][:].rearrange("p (t s) j -> p t s j", t=TILES)[:, tiles],
+                in_=w_raw[q][:].rearrange("p j (s t) -> p t s j", t=TILES)[:, tiles],
+            )
+
+        def quantize_w(q, t):
+            cols = slice(t * P, (t + 1) * P)
+            nc.vector.quantize_mx(
+                out=w_codes[q][:, cols].bitcast(FP8X4),
+                scales=w_scales[q][:, cols],
+                in_=w_bf[q][:, cols, :].rearrange("p m j -> p (m j)"),
+            )
+
+        def multiply(g):
+            q, c = divmod(g, SIDE)
+            rows = slice(c * ROWS, (c + 1) * ROWS)
+            for t in range(TILES):
+                cols = slice(t * P, (t + 1) * P)
+                nc.tensor.matmul_mx(
+                    out=sums[g][t][:],
+                    lhsT=w_codes[q][rows, cols].bitcast(FP8X4),
+                    lhsT_scale=w_scales[q][rows, cols],
+                    rhs=x_codes[q][rows, :].bitcast(FP8X4),
+                    rhs_scale=x_scales[q][rows, :],
+                    start=True,
+                    stop=True,
+                )
+
+        def gelu(g):
+            for t in range(TILES):
+                nc.scalar.activation(out=act[g][:, t, :], in_=sums[g][t][:], func=GELU, bias=bias[:, g, t : t + 1])
+
+        def finish(g):
+            nc.vector.tensor_add(out=act[g][:], in0=act[g][:], in1=res[g][:])
+            nc.sync.dma_start(out=out_rows[g], in_=act[g][:])
+
+        nc.scalar.dma_start(out=bias[:, :, 0:TILES], in_=b_rows)
+        for q in range(PAIRS):
+            nc.sync.dma_start(out=x_raw[q][:], in_=x_rows[q])
+            nc.sync.dma_start(out=w_raw[q][:], in_=w_rows[q])
+        for g in range(G):
+            nc.sync.dma_start(out=res[g][:], in_=r_rows[g])
+
+        left, right = slice(0, N // 2), slice(N // 2, N)
+        pack_x(0, slice(0, N))
+        pack_w(0, slice(0, TILES), nc.vector.tensor_copy)
+        quantize_x(0, slice(0, N))
+        quantize_w(0, 0)
+        quantize_w(0, 1)
+        multiply(0)
+        multiply(1)
+        gelu(0)
+        pack_x(1, left)
+        pack_x(1, right)
+        quantize_x(1, left)
+        quantize_x(1, right)
+        pack_w(1, slice(0, 1), nc.scalar.copy)
+        pack_w(1, slice(1, 2), nc.vector.tensor_copy)
+        quantize_w(1, 0)
+        quantize_w(1, 1)
+        multiply(2)
+        multiply(3)
+        finish(0)
+        for g in range(1, G):
+            gelu(g)
+            finish(g)

@@ -17,7 +17,8 @@ ROWS = D // PACK
 SIDE = P // ROWS
 PAIRS = G // SIDE
 TILES = M // P
-BIAS_PITCH = 8
+QUAD = 32
+X_VECTOR = 320
 
 FLOPS = 2 * G * D * M * N
 
@@ -26,7 +27,7 @@ def tile_rows_glin_gelu_bias_res_kernel(tc, x, w, b, r, out):
     nc = tc.nc
     x_rows = x.flatten_outer_dims().rearrange("(q p j) n -> q p j n", p=P, j=PACK)
     w_rows = w.flatten_outer_dims().rearrange("(q p j) m -> q p j m", p=P, j=PACK)
-    b_rows = b.rearrange("g (p t) o -> p g (t o)", t=TILES)
+    b_rows = b.rearrange("g (u e) o -> u g (e o)", u=P // QUAD)
     r_rows = r.rearrange("g (p t) n -> g p t n", t=TILES)
     out_rows = out.rearrange("g (p t) n -> g p t n", t=TILES)
 
@@ -35,7 +36,10 @@ def tile_rows_glin_gelu_bias_res_kernel(tc, x, w, b, r, out):
         ps = ctx.enter_context(tc.psum_pool(name="ps", bufs=1))
         ctx.enter_context(tc.manual_schedule())
 
-        bias = sb.tile([P, G, BIAS_PITCH], F32, name="bias")
+        b_raw = sb.tile([P, G, QUAD * TILES], F32, name="b_raw", align_bytes=64)
+        b_split = sb.tile([P, G, TILES, QUAD], F32, name="b_split", align_bytes=64)
+        bias = sb.tile([P, G, TILES, QUAD], F32, name="bias", align_bytes=64)
+        warm = sb.tile([P, 1], F32, name="warm")
         x_raw = [sb.tile([P, PACK, N], F32, name="x_raw%d" % q, align_bytes=64) for q in range(PAIRS)]
         w_raw = [sb.tile([P, PACK, M], F32, name="w_raw%d" % q, align_bytes=64) for q in range(PAIRS)]
         x_bf = [sb.tile([P, N, PACK], BF16, name="x_bf%d" % q, align_bytes=64) for q in range(PAIRS)]
@@ -48,8 +52,8 @@ def tile_rows_glin_gelu_bias_res_kernel(tc, x, w, b, r, out):
         act = [sb.tile([P, TILES, N], F32, name="act%d" % g, align_bytes=64) for g in range(G)]
         sums = [[ps.tile([P, N], F32, name="sums%d_%d" % (g, t)) for t in range(TILES)] for g in range(G)]
 
-        def pack_x(q, cols):
-            nc.vector.tensor_copy(out=x_bf[q][:, cols, :], in_=x_raw[q][:, :, cols].rearrange("p j n -> p n j"))
+        def pack_x(q, cols, copy):
+            copy(out=x_bf[q][:, cols, :], in_=x_raw[q][:, :, cols].rearrange("p j n -> p n j"))
 
         def quantize_x(q, cols):
             nc.vector.quantize_mx(
@@ -87,41 +91,52 @@ def tile_rows_glin_gelu_bias_res_kernel(tc, x, w, b, r, out):
                     stop=True,
                 )
 
-        def gelu(g):
-            for t in range(TILES):
-                nc.scalar.activation(out=act[g][:, t, :], in_=sums[g][t][:], func=GELU, bias=bias[:, g, t : t + 1])
+        def gelu(g, t):
+            nc.scalar.activation(out=act[g][:, t, :], in_=sums[g][t][:], func=GELU, bias=bias[:, g, t, 0:1])
 
-        def finish(g):
-            nc.vector.tensor_add(out=act[g][:], in0=act[g][:], in1=res[g][:])
-            nc.sync.dma_start(out=out_rows[g], in_=act[g][:])
+        def add_residual(g, t):
+            nc.vector.tensor_add(out=act[g][:, t, :], in0=act[g][:, t, :], in1=res[g][:, t, :])
 
-        nc.scalar.dma_start(out=bias[:, :, 0:TILES], in_=b_rows)
-        for q in range(PAIRS):
-            nc.sync.dma_start(out=x_raw[q][:], in_=x_rows[q])
-            nc.sync.dma_start(out=w_raw[q][:], in_=w_rows[q])
+        nc.vector.memset(b_raw[:], 0.0)
+        nc.vector.memset(warm[:], 0.0)
+        nc.scalar.activation(out=warm[:], in_=warm[:], func=GELU)
+        nc.sync.dma_start(out=x_raw[0][:], in_=x_rows[0])
+        nc.sync.dma_start(out=b_raw[0:P:QUAD], in_=b_rows)
+        nc.sync.dma_start(out=w_raw[0][:], in_=w_rows[0])
+        nc.sync.dma_start(out=x_raw[1][:], in_=x_rows[1])
+        nc.sync.dma_start(out=w_raw[1][:], in_=w_rows[1])
         for g in range(G):
             nc.sync.dma_start(out=res[g][:], in_=r_rows[g])
 
-        left, right = slice(0, N // 2), slice(N // 2, N)
-        pack_x(0, slice(0, N))
-        pack_w(0, slice(0, TILES), nc.vector.tensor_copy)
-        quantize_x(0, slice(0, N))
-        quantize_w(0, 0)
-        quantize_w(0, 1)
+        def prepare_x(q):
+            pack_x(q, slice(0, N // 2), nc.vector.tensor_copy)
+            pack_x(q, slice(N // 2, X_VECTOR), nc.vector.tensor_copy)
+            pack_x(q, slice(X_VECTOR, N), nc.scalar.copy)
+            quantize_x(q, slice(0, N // 2))
+            quantize_x(q, slice(N // 2, N))
+
+        def prepare_w(q):
+            pack_w(q, slice(0, 1), nc.scalar.copy)
+            pack_w(q, slice(1, 2), nc.vector.tensor_copy)
+            quantize_w(q, 0)
+            quantize_w(q, 1)
+
+        prepare_x(0)
+        prepare_w(0)
+        nc.scalar.copy(out=b_split[:], in_=b_raw[:].rearrange("p g (i t) -> p g t i", t=TILES))
+        nc.vector.transpose(
+            out=bias[:].rearrange("p g t i -> p (g t i)"), in_=b_split[:].rearrange("p g t i -> p (g t i)")
+        )
         multiply(0)
         multiply(1)
-        gelu(0)
-        pack_x(1, left)
-        pack_x(1, right)
-        quantize_x(1, left)
-        quantize_x(1, right)
-        pack_w(1, slice(0, 1), nc.scalar.copy)
-        pack_w(1, slice(1, 2), nc.vector.tensor_copy)
-        quantize_w(1, 0)
-        quantize_w(1, 1)
+        gelu(0, 0)
+        prepare_x(1)
+        prepare_w(1)
         multiply(2)
         multiply(3)
-        finish(0)
-        for g in range(1, G):
-            gelu(g)
-            finish(g)
+        for g in range(G):
+            for t in range(TILES):
+                if (g, t) != (0, 0):
+                    gelu(g, t)
+                add_residual(g, t)
+            nc.sync.dma_start(out=out_rows[g], in_=act[g][:])

@@ -19,6 +19,7 @@ PAIRS = G // SIDE
 TILES = M // P
 QUAD = 32
 X_VECTOR = 320
+RUN = 2
 
 FLOPS = 2 * G * D * M * N
 
@@ -53,7 +54,10 @@ def tile_rows_glin_gelu_bias_res_kernel(tc, x, w, b, r, out):
         sums = [[ps.tile([P, N], F32, name="sums%d_%d" % (g, t)) for t in range(TILES)] for g in range(G)]
 
         def pack_x(q, cols, copy):
-            copy(out=x_bf[q][:, cols, :], in_=x_raw[q][:, :, cols].rearrange("p j n -> p n j"))
+            copy(
+                out=x_bf[q][:, cols, :].rearrange("p (n i) j -> p n j i", i=RUN),
+                in_=x_raw[q][:, :, cols].rearrange("p j (n i) -> p n j i", i=RUN),
+            )
 
         def quantize_x(q, cols):
             nc.vector.quantize_mx(
@@ -62,10 +66,10 @@ def tile_rows_glin_gelu_bias_res_kernel(tc, x, w, b, r, out):
                 in_=x_bf[q][:, cols, :].rearrange("p n j -> p (n j)"),
             )
 
-        def pack_w(q, tiles, copy):
+        def pack_w(q, slots, copy):
             copy(
-                out=w_bf[q][:].rearrange("p (t s) j -> p t s j", t=TILES)[:, tiles],
-                in_=w_raw[q][:].rearrange("p j (s t) -> p t s j", t=TILES)[:, tiles],
+                out=w_bf[q][:].rearrange("p (t s) j -> p s j t", t=TILES)[:, slots],
+                in_=w_raw[q][:].rearrange("p j (s t) -> p s j t", t=TILES)[:, slots],
             )
 
         def quantize_w(q, t):
@@ -108,21 +112,19 @@ def tile_rows_glin_gelu_bias_res_kernel(tc, x, w, b, r, out):
         for g in range(G):
             nc.sync.dma_start(out=res[g][:], in_=r_rows[g])
 
-        def prepare_x(q):
-            pack_x(q, slice(0, N // 2), nc.vector.tensor_copy)
-            pack_x(q, slice(N // 2, X_VECTOR), nc.vector.tensor_copy)
+        def prepare(q):
+            left, right = slice(0, N // 2), slice(N // 2, N)
             pack_x(q, slice(X_VECTOR, N), nc.scalar.copy)
-            quantize_x(q, slice(0, N // 2))
-            quantize_x(q, slice(N // 2, N))
+            pack_w(q, slice(0, P // 2), nc.scalar.copy)
+            pack_x(q, left, nc.vector.tensor_copy)
+            pack_x(q, slice(N // 2, X_VECTOR), nc.vector.tensor_copy)
+            quantize_x(q, left)
+            pack_w(q, slice(P // 2, P), nc.vector.tensor_copy)
+            quantize_x(q, right)
+            for t in range(TILES):
+                quantize_w(q, t)
 
-        def prepare_w(q):
-            pack_w(q, slice(0, 1), nc.scalar.copy)
-            pack_w(q, slice(1, 2), nc.vector.tensor_copy)
-            quantize_w(q, 0)
-            quantize_w(q, 1)
-
-        prepare_x(0)
-        prepare_w(0)
+        prepare(0)
         nc.scalar.copy(out=b_split[:], in_=b_raw[:].rearrange("p g (i t) -> p g t i", t=TILES))
         nc.vector.transpose(
             out=bias[:].rearrange("p g t i -> p (g t i)"), in_=b_split[:].rearrange("p g t i -> p (g t i)")
@@ -130,8 +132,7 @@ def tile_rows_glin_gelu_bias_res_kernel(tc, x, w, b, r, out):
         multiply(0)
         multiply(1)
         gelu(0, 0)
-        prepare_x(1)
-        prepare_w(1)
+        prepare(1)
         multiply(2)
         multiply(3)
         for g in range(G):

@@ -37,20 +37,20 @@ def tile_rows_glin_gelu_bias_res_kernel(tc, x, w, b, r, out):
         ps = ctx.enter_context(tc.psum_pool(name="ps", bufs=1))
         ctx.enter_context(tc.manual_schedule())
 
-        b_raw = sb.tile([P, G, QUAD * TILES], F32, name="b_raw", align_bytes=64)
-        b_split = sb.tile([P, G, TILES, QUAD], F32, name="b_split", align_bytes=64)
-        bias = sb.tile([P, G, TILES, QUAD], F32, name="bias", align_bytes=64)
+        b_raw = sb.tile([P, G, QUAD * TILES], F32, name="b_raw", align_bytes=256)
+        b_split = sb.tile([P, G, TILES, QUAD], F32, name="b_split", align_bytes=256)
+        bias = sb.tile([P, G, TILES, QUAD], F32, name="bias", align_bytes=256)
         warm = sb.tile([P, 1], F32, name="warm")
-        x_raw = [sb.tile([P, PACK, N], F32, name="x_raw%d" % q, align_bytes=64) for q in range(PAIRS)]
-        w_raw = [sb.tile([P, PACK, M], F32, name="w_raw%d" % q, align_bytes=64) for q in range(PAIRS)]
-        x_bf = [sb.tile([P, N, PACK], BF16, name="x_bf%d" % q, align_bytes=64) for q in range(PAIRS)]
-        w_bf = [sb.tile([P, M, PACK], BF16, name="w_bf%d" % q, align_bytes=64) for q in range(PAIRS)]
-        x_codes = [sb.tile([P, N], U32, name="x_codes%d" % q, align_bytes=64) for q in range(PAIRS)]
-        w_codes = [sb.tile([P, M], U32, name="w_codes%d" % q, align_bytes=64) for q in range(PAIRS)]
-        x_scales = [sb.tile([P, N], U8, name="x_scales%d" % q, align_bytes=64) for q in range(PAIRS)]
-        w_scales = [sb.tile([P, M], U8, name="w_scales%d" % q, align_bytes=64) for q in range(PAIRS)]
-        res = [sb.tile([P, TILES, N], F32, name="res%d" % g, align_bytes=64) for g in range(G)]
-        act = [sb.tile([P, TILES, N], F32, name="act%d" % g, align_bytes=64) for g in range(G)]
+        x_raw = [sb.tile([P, PACK, N], F32, name="x_raw%d" % q, align_bytes=256) for q in range(PAIRS)]
+        w_raw = [sb.tile([P, PACK, M], F32, name="w_raw%d" % q, align_bytes=256) for q in range(PAIRS)]
+        x_bf = [sb.tile([P, N, PACK], BF16, name="x_bf%d" % q, align_bytes=256) for q in range(PAIRS)]
+        w_bf = [sb.tile([P, M, PACK], BF16, name="w_bf%d" % q, align_bytes=256) for q in range(PAIRS)]
+        x_codes = [sb.tile([P, N], U32, name="x_codes%d" % q, align_bytes=256) for q in range(PAIRS)]
+        w_codes = [sb.tile([P, M], U32, name="w_codes%d" % q, align_bytes=256) for q in range(PAIRS)]
+        x_scales = [sb.tile([P, N], U8, name="x_scales%d" % q, align_bytes=256) for q in range(PAIRS)]
+        w_scales = [sb.tile([P, M], U8, name="w_scales%d" % q, align_bytes=256) for q in range(PAIRS)]
+        res = [sb.tile([P, TILES, N], F32, name="res%d" % g, align_bytes=256) for g in range(G)]
+        act = [sb.tile([P, TILES, N], F32, name="act%d" % g, align_bytes=256) for g in range(G)]
         sums = [[ps.tile([P, N], F32, name="sums%d_%d" % (g, t)) for t in range(TILES)] for g in range(G)]
 
         def pack_x(q, cols, copy):

@@ -19,6 +19,7 @@ PAIRS = G // SIDE
 TILES = M // P
 QUAD = 32
 X_VECTOR = 320
+W_SCALAR = 44
 RUN = 2
 
 FLOPS = 2 * G * D * M * N
@@ -115,17 +116,18 @@ def tile_rows_glin_gelu_bias_res_kernel(tc, x, w, b, r, out):
         def prepare(q):
             left, right = slice(0, N // 2), slice(N // 2, N)
             pack_x(q, slice(X_VECTOR, N), nc.scalar.copy)
-            pack_w(q, slice(0, P // 2), nc.scalar.copy)
+            if q == 0:
+                nc.scalar.copy(out=b_split[:], in_=b_raw[:].rearrange("p g (i t) -> p g t i", t=TILES))
+            pack_w(q, slice(0, W_SCALAR), nc.scalar.copy)
             pack_x(q, left, nc.vector.tensor_copy)
             pack_x(q, slice(N // 2, X_VECTOR), nc.vector.tensor_copy)
             quantize_x(q, left)
-            pack_w(q, slice(P // 2, P), nc.vector.tensor_copy)
+            pack_w(q, slice(W_SCALAR, P), nc.vector.tensor_copy)
             quantize_x(q, right)
             for t in range(TILES):
                 quantize_w(q, t)
 
         prepare(0)
-        nc.scalar.copy(out=b_split[:], in_=b_raw[:].rearrange("p g (i t) -> p g t i", t=TILES))
         nc.vector.transpose(
             out=bias[:].rearrange("p g t i -> p (g t i)"), in_=b_split[:].rearrange("p g t i -> p (g t i)")
         )

@@ -106,7 +106,8 @@ def tile_rows_glin_gelu_bias_res_kernel(tc, x, w, b, r, out):
         nc.vector.memset(warm[:], 0.0)
         nc.scalar.activation(out=warm[:], in_=warm[:], func=GELU)
         nc.sync.dma_start(out=x_raw[0][:], in_=x_rows[0])
-        nc.sync.dma_start(out=b_raw[0:P:QUAD], in_=b_rows)
+        for g in range(G):
+            nc.sync.dma_start(out=b_raw[0:P:QUAD, g, :], in_=b_rows[:, g, :])
         nc.sync.dma_start(out=w_raw[0][:], in_=w_rows[0])
         nc.sync.dma_start(out=x_raw[1][:], in_=x_rows[1])
         nc.sync.dma_start(out=w_raw[1][:], in_=w_rows[1])

@@ -134,13 +134,11 @@ def tile_rows_glin_gelu_bias_res_kernel(tc, x, w, b, r, out):
         )
         multiply(0)
         multiply(1)
-        gelu(0, 0)
         prepare(1)
         multiply(2)
         multiply(3)
         for g in range(G):
             for t in range(TILES):
-                if (g, t) != (0, 0):
-                    gelu(g, t)
+                gelu(g, t)
                 add_residual(g, t)
             nc.sync.dma_start(out=out_rows[g], in_=act[g][:])

@@ -141,4 +141,7 @@ def tile_rows_glin_gelu_bias_res_kernel(tc, x, w, b, r, out):
             for t in range(TILES):
                 gelu(g, t)
                 add_residual(g, t)
-            nc.sync.dma_start(out=out_rows[g], in_=act[g][:])
+            if g == 1:
+                nc.scalar.dma_start(out=out_rows[0], in_=act[0][:])
+            if g > 0:
+                nc.sync.dma_start(out=out_rows[g], in_=act[g][:])

from contextlib import ExitStack

import concourse.mybir as mybir

G, D, M, N = 4, 256, 256, 512

F32 = mybir.dt.float32
BF16 = mybir.dt.bfloat16
U32 = mybir.dt.uint32
U8 = mybir.dt.uint8
FP8X4 = mybir.dt.float8_e4m3fn_x4
GELU = mybir.ActivationFunctionType.Gelu_apprx_tanh

P = 128
PACK = 4
ROWS = D // PACK
SIDE = P // ROWS
PAIRS = G // SIDE
TILES = M // P
QUAD = 32
X_VECTOR = 320
W_SCALAR = 44
RUN = 2

FLOPS = 2 * G * D * M * N


def tile_rows_glin_gelu_bias_res_kernel(tc, x, w, b, r, out):
    nc = tc.nc
    x_rows = x.flatten_outer_dims().rearrange("(q p j) n -> q p j n", p=P, j=PACK)
    w_rows = w.flatten_outer_dims().rearrange("(q p j) m -> q p j m", p=P, j=PACK)
    b_rows = b.rearrange("g (u e) o -> u g (e o)", u=P // QUAD)
    r_rows = r.rearrange("g (p t) n -> g p t n", t=TILES)
    out_rows = out.rearrange("g (p t) n -> g p t n", t=TILES)

    with ExitStack() as ctx:
        sb = ctx.enter_context(tc.tile_pool(name="sb", bufs=1))
        ps = ctx.enter_context(tc.psum_pool(name="ps", bufs=1))
        ctx.enter_context(tc.manual_schedule())

        b_raw = sb.tile([P, G, QUAD * TILES], F32, name="b_raw", align_bytes=256)
        b_split = sb.tile([P, G, TILES, QUAD], F32, name="b_split", align_bytes=256)
        bias = sb.tile([P, G, TILES, QUAD], F32, name="bias", align_bytes=256)
        warm = sb.tile([P, 1], F32, name="warm")
        x_raw = [sb.tile([P, PACK, N], F32, name="x_raw%d" % q, align_bytes=256) for q in range(PAIRS)]
        w_raw = [sb.tile([P, PACK, M], F32, name="w_raw%d" % q, align_bytes=256) for q in range(PAIRS)]
        x_bf = [sb.tile([P, N, PACK], BF16, name="x_bf%d" % q, align_bytes=256) for q in range(PAIRS)]
        w_bf = [sb.tile([P, M, PACK], BF16, name="w_bf%d" % q, align_bytes=256) for q in range(PAIRS)]
        x_codes = [sb.tile([P, N], U32, name="x_codes%d" % q, align_bytes=256) for q in range(PAIRS)]
        w_codes = [sb.tile([P, M], U32, name="w_codes%d" % q, align_bytes=256) for q in range(PAIRS)]
        x_scales = [sb.tile([P, N], U8, name="x_scales%d" % q, align_bytes=256) for q in range(PAIRS)]
        w_scales = [sb.tile([P, M], U8, name="w_scales%d" % q, align_bytes=256) for q in range(PAIRS)]
        res = [sb.tile([P, TILES, N], F32, name="res%d" % g, align_bytes=256) for g in range(G)]
        act = [sb.tile([P, TILES, N], F32, name="act%d" % g, align_bytes=256) for g in range(G)]
        sums = [[ps.tile([P, N], F32, name="sums%d_%d" % (g, t)) for t in range(TILES)] for g in range(G)]

        def pack_x(q, cols, copy):
            copy(
                out=x_bf[q][:, cols, :].rearrange("p (n i) j -> p n j i", i=RUN),
                in_=x_raw[q][:, :, cols].rearrange("p j (n i) -> p n j i", i=RUN),
            )

        def quantize_x(q, cols):
            nc.vector.quantize_mx(
                out=x_codes[q][:, cols].bitcast(FP8X4),
                scales=x_scales[q][:, cols],
                in_=x_bf[q][:, cols, :].rearrange("p n j -> p (n j)"),
            )

        def pack_w(q, slots, copy):
            copy(
                out=w_bf[q][:].rearrange("p (t s) j -> p s j t", t=TILES)[:, slots],
                in_=w_raw[q][:].rearrange("p j (s t) -> p s j t", t=TILES)[:, slots],
            )

        def quantize_w(q, t):
            cols = slice(t * P, (t + 1) * P)
            nc.vector.quantize_mx(
                out=w_codes[q][:, cols].bitcast(FP8X4),
                scales=w_scales[q][:, cols],
                in_=w_bf[q][:, cols, :].rearrange("p m j -> p (m j)"),
            )

        def multiply(g):
            q, c = divmod(g, SIDE)
            rows = slice(c * ROWS, (c + 1) * ROWS)
            for t in range(TILES):
                cols = slice(t * P, (t + 1) * P)
                nc.tensor.matmul_mx(
                    out=sums[g][t][:],
                    lhsT=w_codes[q][rows, cols].bitcast(FP8X4),
                    lhsT_scale=w_scales[q][rows, cols],
                    rhs=x_codes[q][rows, :].bitcast(FP8X4),
                    rhs_scale=x_scales[q][rows, :],
                    start=True,
                    stop=True,
                )

        def gelu(g, t):
            nc.scalar.activation(out=act[g][:, t, :], in_=sums[g][t][:], func=GELU, bias=bias[:, g, t, 0:1])

        def add_residual(g, t):
            nc.vector.tensor_add(out=act[g][:, t, :], in0=act[g][:, t, :], in1=res[g][:, t, :])

        nc.vector.memset(b_raw[:], 0.0)
        nc.vector.memset(warm[:], 0.0)
        nc.scalar.activation(out=warm[:], in_=warm[:], func=GELU)
        nc.sync.dma_start(out=x_raw[0][:], in_=x_rows[0])
        for g in range(G):
            nc.sync.dma_start(out=b_raw[0:P:QUAD, g, :], in_=b_rows[:, g, :])
        nc.sync.dma_start(out=w_raw[0][:], in_=w_rows[0])
        nc.sync.dma_start(out=x_raw[1][:], in_=x_rows[1])
        nc.sync.dma_start(out=w_raw[1][:], in_=w_rows[1])
        for g in range(G):
            nc.sync.dma_start(out=res[g][:], in_=r_rows[g])

        def prepare(q):
            left, right = slice(0, N // 2), slice(N // 2, N)
            pack_x(q, slice(X_VECTOR, N), nc.scalar.copy)
            if q == 0:
                nc.scalar.copy(out=b_split[:], in_=b_raw[:].rearrange("p g (i t) -> p g t i", t=TILES))
            pack_w(q, slice(0, W_SCALAR), nc.scalar.copy)
            pack_x(q, left, nc.vector.tensor_copy)
            pack_x(q, slice(N // 2, X_VECTOR), nc.vector.tensor_copy)
            quantize_x(q, left)
            pack_w(q, slice(W_SCALAR, P), nc.vector.tensor_copy)
            quantize_x(q, right)
            for t in range(TILES):
                quantize_w(q, t)

        prepare(0)
        nc.vector.transpose(
            out=bias[:].rearrange("p g t i -> p (g t i)"), in_=b_split[:].rearrange("p g t i -> p (g t i)")
        )
        multiply(0)
        multiply(1)
        prepare(1)
        multiply(2)
        multiply(3)
        for g in range(G):
            for t in range(TILES):
                gelu(g, t)
                add_residual(g, t)
            if g == 1:
                nc.scalar.dma_start(out=out_rows[0], in_=act[0][:])
            if g > 0:
                nc.sync.dma_start(out=out_rows[g], in_=act[g][:])
